import numpy as np
import ml_dtypes


def mxq(x, axis, fmt="e4m3"):
    dtype, down = {"e4m3": (ml_dtypes.float8_e4m3fn, 7), "e5m2": (ml_dtypes.float8_e5m2, 14)}[fmt]
    v = np.moveaxis(np.asarray(x, np.float32).astype(ml_dtypes.bfloat16).astype(np.float64), axis, -1)
    blocks = v.reshape(v.shape[:-1] + (-1, 32))
    amax = np.abs(blocks).max(-1, keepdims=True)
    byte = np.maximum(np.where(amax > 0, np.frexp(amax)[1] - 1 + 127, 0) - down, 1)
    scale = np.exp2(byte - 127.0)
    codes = (blocks / scale).astype(np.float32).astype(dtype).astype(np.float64)
    return np.moveaxis((codes * scale).reshape(v.shape), -1, axis)


WIDE = False


def mx_kscale(k):
    if not WIDE:
        return np.ones(k)
    levels = np.array([10, -10, 5, -5, 0])
    if k % 512:
        return np.exp2(np.random.permutation(np.resize(levels, k // 32))).repeat(32)
    a = np.empty((k // 512, 16))
    for p in range(k // 512):
        a[p, :8] = np.random.permutation(np.resize(levels, 8))
        for g in range(8):
            far = levels[np.abs(levels - a[p, g]) >= 10]
            a[p, g + 8] = far[np.random.randint(len(far))]
    return np.exp2(a.ravel()).repeat(32)


def f64(x):
    return np.asarray(x).astype(np.float64)


def striped8(idx):
    return np.asarray(idx).reshape(8, -1, 16).transpose(0, 2, 1).reshape(128, -1).astype(np.uint16)


def unstriped8(offs):
    return offs.reshape(8, 16, -1).transpose(0, 2, 1).reshape(8, -1).astype(np.int64)


def pick8(x, idx, run):
    r = np.arange(len(x))
    return x[r[:, None], idx[r % (8 * run) // run]]


E2M1 = np.array([0.0, 0.5, 1.0, 1.5, 2.0, 3.0, 4.0, 6.0, -0.0, -0.5, -1.0, -1.5, -2.0, -3.0, -4.0, -6.0])


def pack_weight(w, fmt):
    k, n = w.shape
    w = f64(np.asarray(w, np.float32).astype(ml_dtypes.bfloat16)).reshape(k // 32, 32, n)
    amax = np.abs(w).max(1)
    if fmt == "e4m3":
        byte = np.frexp(amax)[1] - 1 + 127 - 7
    else:
        mant, ex = np.frexp(amax / 6.0)
        byte = np.where(mant > 0.5, ex, ex - 1) + 127
    byte = np.clip(np.where(amax > 0, byte, 1), 1, 254)
    scaled = (w * np.exp2(127.0 - byte)[:, None, :]).reshape(k, n).astype(np.float32)
    by_word = np.ascontiguousarray(scaled.reshape(k // 512, 128, 4, n).transpose(0, 1, 3, 2))
    if fmt == "e4m3":
        words = by_word.astype(ml_dtypes.float8_e4m3fn).view(np.uint8)
    else:
        c = by_word.astype(ml_dtypes.float4_e2m1fn).view(np.uint8) & 0xF
        words = (c[..., 0::2] | (c[..., 1::2] << 4)).reshape(k // 512, 128, 2 * n)
    return np.ascontiguousarray(words), np.ascontiguousarray(byte.astype(np.uint8).reshape(k // 512, 16, n))


def unpack_weight(words, scales, fmt):
    g, _, n = scales.shape
    words = np.ascontiguousarray(words).reshape(g, 128, n, -1)
    if fmt == "e4m3":
        vals = words.view(ml_dtypes.float8_e4m3fn).astype(np.float64)
    else:
        nib = np.empty((g, 128, n, 4), np.uint8)
        nib[..., 0::2] = words & 0xF
        nib[..., 1::2] = words >> 4
        vals = E2M1[nib]
    vals = vals * np.repeat(np.exp2(scales.astype(np.float64) - 127.0), 8, axis=1)[..., None]
    return vals.transpose(0, 1, 3, 2).reshape(g * 512, n)


def softplus(v):
    return np.log(1.0 + np.exp(v))


D, T, I, Q = 512, 1024, 512, 128


def setup_inputs():
    n = np.random.standard_normal
    idx = np.stack([np.random.permutation(T)[:I] for _ in range(8)])
    idx2 = np.stack([np.random.permutation(T)[:I] for _ in range(8)])
    idx3 = np.stack([np.random.permutation(T)[:I] for _ in range(8)])
    fd = mx_kscale(D)
    keysp = pack_weight(n((D, T)) / fd[:, None], "e4m3")
    return {
        "query": (n((D, Q)) * 0.9 / np.sqrt(D) * fd[:, None]).astype(np.float32),
        "query2": (n((D, Q)) * 0.9 / np.sqrt(D) * fd[:, None]).astype(np.float32),
        "keys_words": keysp[0],
        "keys_scales": keysp[1],
        "lam": (np.random.uniform(0.6, 1.2, (Q, 1))).astype(np.float32),
        "old": (1.0 * n((Q, T))).astype(np.float32),
        "offs": striped8(idx),
        "offs2": striped8(idx2),
        "offs3": striped8(idx3),
    }


def reference(query, query2, keys_words, keys_scales, lam, old, offs, offs2, offs3):
    idx = unstriped8(offs)
    idx2 = unstriped8(offs2)
    idx3 = unstriped8(offs3)
    keysu = unpack_weight(keys_words, keys_scales, "e4m3")
    queryq = mxq(f64(query), 0, "e4m3")
    a = queryq.T @ keysu
    query2q = mxq(f64(query2), 0, "e4m3")
    b = query2q.T @ keysu
    w = pick8(a, idx, 16) / (softplus(pick8(b, idx2, 16)) + 0.5) * f64(lam)
    f1 = np.zeros((Q, T))
    f1[np.arange(Q)[:, None], idx[np.arange(Q) % 128 // 16]] = w
    f2 = f1 + f64(old)
    y = pick8(f2, idx3, 16) * w
    return y

@@ -1,0 +1,161 @@
+from contextlib import ExitStack
+
+import concourse.mybir as mybir
+
+F32 = mybir.dt.float32
+BF16 = mybir.dt.bfloat16
+I32 = mybir.dt.int32
+U32 = mybir.dt.uint32
+U16 = mybir.dt.uint16
+U8 = mybir.dt.uint8
+FP8X4 = mybir.dt.float8_e4m3fn_x4
+ALU = mybir.AluOpType
+ACT = mybir.ActivationFunctionType
+
+D, T, I, Q = 512, 1024, 512, 128
+P = 128
+PACK = 4
+N_PASS = 256
+PASSES = T // N_PASS
+HALF = I // 2
+FIRST = 128
+TINY = 2.0 ** -60
+
+FLOPS = 2 * 2 * D * T * Q
+
+
+def entries(offsets, start, stop):
+    return offsets[:, start // 16 : stop // 16]
+
+
+def tile_attend_worthfor_lean_throughtimes_heads_kernel(
+    tc, query, query2, keys_words, keys_scales, lam, old, offs, offs2, offs3, out
+):
+    nc = tc.nc
+    with ExitStack() as ctx:
+        sb = ctx.enter_context(tc.tile_pool(name="sb", bufs=1))
+        ps = ctx.enter_context(tc.psum_pool(name="ps", bufs=1))
+
+        key_scale = sb.tile([P, N_PASS], U8, name="key_scale", align_bytes=64)
+
+        q2_raw = sb.tile([P, PACK, Q], F32, name="q2_raw")
+        nc.sync.dma_start(out=q2_raw[:], in_=query2.rearrange("(p j) q -> p j q", j=PACK))
+        scale_rows = keys_scales[0].bitcast(I32)
+        for quad in range(4):
+            nc.sync.dma_start(
+                out=key_scale[32 * quad : 32 * quad + 16, :].bitcast(I32),
+                in_=scale_rows[4 * quad : 4 * quad + 4, :].rearrange("j (h c) -> h j c", h=PASSES),
+            )
+        key_words = sb.tile([P, T], U32, name="key_words", align_bytes=64)
+        words = keys_words[0].rearrange("p n t -> p (n t)").bitcast(I32)
+        nc.sync.dma_start(out=key_words[:, : T // 2].bitcast(I32), in_=words[:, : T // 2])
+        nc.sync.dma_start(out=key_words[:, T // 2 :].bitcast(I32), in_=words[:, T // 2 :])
+        q_raw = sb.tile([P, PACK, Q], F32, name="q_raw")
+        nc.sync.dma_start(out=q_raw[:], in_=query.rearrange("(p j) q -> p j q", j=PACK))
+        list_b = sb.tile([P, I // 16], U16, name="list_b")
+        nc.sync.dma_start(list_b[:], offs2)
+        list_a = sb.tile([P, I // 16], U16, name="list_a")
+        nc.sync.dma_start(list_a[:], offs)
+        lam_sb = sb.tile([P, 1], F32, name="lam_sb")
+        nc.sync.dma_start(out=lam_sb[:], in_=lam)
+        old_sb = sb.tile([P, T], F32, name="old_sb")
+        nc.sync.dma_start(out=old_sb[:], in_=old)
+        list_f = sb.tile([P, I // 16], U16, name="list_f")
+        nc.sync.dma_start(list_f[:], offs3)
+
+        f1 = sb.tile([P, T], F32, name="f1")
+        nc.gpsimd.memset(f1[:], 0.0)
+
+        def quantise(raw, name, cast):
+            grouped = sb.tile(
+                [P, Q, PACK], BF16, name=name + "_grouped", tag=name + "_grouped", align_bytes=64
+            )
+            cast(
+                grouped[:].rearrange("p (c i) t -> p c t i", i=4),
+                raw[:].rearrange("p t (c i) -> p c t i", i=4),
+            )
+            codes = sb.tile([P, Q], U32, name=name + "_codes", align_bytes=64)
+            scale = sb.tile([P, Q], U8, name=name + "_scale", align_bytes=64)
+            nc.vector.quantize_mx(
+                out=codes[:].bitcast(FP8X4),
+                scales=scale[:],
+                in_=grouped[:].rearrange("p q t -> p (q t)"),
+            )
+            return codes, scale
+
+        def scores(codes, scale, name, copies, banks):
+            whole = sb.tile([P, T], F32, name=name, tag=name)
+            width = T // len(copies)
+            for n, copy in enumerate(copies):
+                bank = ps.tile([P, width], F32, name=name + "_bank%d" % n, tag="bank%d" % banks[n])
+                for col in range(0, width, N_PASS):
+                    token = n * width + col
+                    nc.tensor.matmul_mx(
+                        out=bank[:, col : col + N_PASS],
+                        lhsT=codes[:].bitcast(FP8X4),
+                        lhsT_scale=scale[:],
+                        rhs=key_words[:, token : token + N_PASS].bitcast(FP8X4),
+                        rhs_scale=key_scale[4 * (token // N_PASS) : P, :],
+                        start=True,
+                        stop=True,
+                    )
+                copy(whole[:, n * width : (n + 1) * width], bank[:])
+            return whole
+
+        q2_codes, q2_scale = quantise(q2_raw, "q2", nc.vector.tensor_copy)
+        q_codes, q_scale = quantise(q_raw, "q", nc.vector.tensor_copy)
+        b_sb = scores(
+            q2_codes, q2_scale, "b_sb", [nc.scalar.copy] * 4, [0, 1, 2, 3]
+        )
+
+        lo, hi = slice(0, HALF), slice(HALF, I)
+        sig = sb.tile([P, I], F32, name="sig")
+        nc.scalar.activation(sig[:], b_sb[:].indirect(list_b[:]), ACT.Sigmoid, scale=-1.0)
+        b_listed = sb.tile([P, I], F32, name="b_listed", tag="q_grouped", align_bytes=64)
+        nc.vector.tensor_copy(b_listed[:], b_sb[:].indirect(list_b[:]))
+
+        a_sb = scores(q_codes, q_scale, "a_sb", [nc.vector.tensor_copy] * 2, [3, 2])
+        a_listed = sb.tile([P, I], F32, name="a_listed")
+        nc.vector.tensor_copy(a_listed[:], a_sb[:].indirect(list_a[:]))
+
+        log_sig = sb.tile([P, I], F32, name="log_sig")
+        nc.scalar.activation(log_sig[:], sig[:], ACT.Ln, bias=TINY)
+        soft = sb.tile([P, I], F32, name="soft", tag="a_sb")
+        den_sq = sb.tile([P, I], F32, name="den_sq")
+        a_lam = sb.tile([P, I], F32, name="a_lam")
+        for part in (lo, hi):
+            nc.vector.scalar_tensor_tensor(
+                soft[:, part], log_sig[:, part], -1.0, b_listed[:, part], ALU.mult, ALU.max
+            )
+        nc.vector.scalar_tensor_tensor(den_sq[:, lo], soft[:, lo], 1.0, soft[:, lo], ALU.add, ALU.mult)
+        nc.vector.tensor_scalar(a_lam[:], a_listed[:], lam_sb[:], None, ALU.mult)
+        nc.vector.scalar_tensor_tensor(den_sq[:, hi], soft[:, hi], 1.0, soft[:, hi], ALU.add, ALU.mult)
+
+        inv_den = sb.tile([P, I], F32, name="inv_den")
+        w = sb.tile([P, I], F32, name="w")
+        for start, stop in ((0, FIRST), (FIRST, I)):
+            nc.scalar.activation(
+                inv_den[:, start:stop], den_sq[:, start:stop], ACT.Abs_reciprocal_sqrt, bias=0.25
+            )
+        nc.vector.tensor_tensor(
+            f1[:].indirect(entries(list_a, 0, FIRST)), a_lam[:, :FIRST], inv_den[:, :FIRST], ALU.mult
+        )
+        nc.vector.tensor_tensor(w[:, lo], a_lam[:, lo], inv_den[:, lo], ALU.mult)
+        nc.vector.tensor_tensor(
+            f1[:].indirect(entries(list_a, FIRST, I)), a_lam[:, FIRST:], inv_den[:, FIRST:], ALU.mult
+        )
+        nc.vector.tensor_tensor(w[:, hi], a_lam[:, hi], inv_den[:, hi], ALU.mult)
+
+        f2 = sb.tile([P, T], F32, name="f2")
+        nc.vector.tensor_tensor(f2[:], f1[:], old_sb[:], ALU.add)
+
+        out_lo = sb.tile([P, HALF], F32, name="out_lo")
+        out_hi = sb.tile([P, HALF], F32, name="out_hi")
+        f2_hi = sb.tile([P, HALF], F32, name="f2_hi")
+        nc.scalar.activation(f2_hi[:], f2[:].indirect(entries(list_f, HALF, I)), ACT.Copy)
+        nc.vector.tensor_tensor(
+            out_lo[:], f2[:].indirect(entries(list_f, 0, HALF)), w[:, lo], ALU.mult
+        )
+        nc.sync.dma_start(out=out[:, lo], in_=out_lo[:])
+        nc.vector.tensor_tensor(out_hi[:], f2_hi[:], w[:, hi], ALU.mult)
+        nc.scalar.dma_start(out=out[:, hi], in_=out_hi[:])

@@ -65,6 +65,10 @@ def tile_attend_worthfor_lean_throughtimes_heads_kernel(
 
         f1 = sb.tile([P, T], F32, name="f1")
         nc.gpsimd.memset(f1[:], 0.0)
+        warm = sb.tile([P, 1], F32, name="warm")
+        nc.vector.memset(warm[:], 0.0)
+        warm_out = sb.tile([P, 1], F32, name="warm_out")
+        nc.scalar.activation(warm_out[:], warm[:], ACT.Sigmoid)
 
         def quantise(raw, name, cast):
             grouped = sb.tile(

from contextlib import ExitStack

import concourse.mybir as mybir

F32 = mybir.dt.float32
BF16 = mybir.dt.bfloat16
I32 = mybir.dt.int32
U32 = mybir.dt.uint32
U16 = mybir.dt.uint16
U8 = mybir.dt.uint8
FP8X4 = mybir.dt.float8_e4m3fn_x4
ALU = mybir.AluOpType
ACT = mybir.ActivationFunctionType

D, T, I, Q = 512, 1024, 512, 128
P = 128
PACK = 4
N_PASS = 256
PASSES = T // N_PASS
HALF = I // 2
FIRST = 128
TINY = 2.0 ** -60

FLOPS = 2 * 2 * D * T * Q


def entries(offsets, start, stop):
    return offsets[:, start // 16 : stop // 16]


def tile_attend_worthfor_lean_throughtimes_heads_kernel(
    tc, query, query2, keys_words, keys_scales, lam, old, offs, offs2, offs3, out
):
    nc = tc.nc
    with ExitStack() as ctx:
        sb = ctx.enter_context(tc.tile_pool(name="sb", bufs=1))
        ps = ctx.enter_context(tc.psum_pool(name="ps", bufs=1))

        key_scale = sb.tile([P, N_PASS], U8, name="key_scale", align_bytes=64)

        q2_raw = sb.tile([P, PACK, Q], F32, name="q2_raw")
        nc.sync.dma_start(out=q2_raw[:], in_=query2.rearrange("(p j) q -> p j q", j=PACK))
        scale_rows = keys_scales[0].bitcast(I32)
        for quad in range(4):
            nc.sync.dma_start(
                out=key_scale[32 * quad : 32 * quad + 16, :].bitcast(I32),
                in_=scale_rows[4 * quad : 4 * quad + 4, :].rearrange("j (h c) -> h j c", h=PASSES),
            )
        key_words = sb.tile([P, T], U32, name="key_words", align_bytes=64)
        words = keys_words[0].rearrange("p n t -> p (n t)").bitcast(I32)
        nc.sync.dma_start(out=key_words[:, : T // 2].bitcast(I32), in_=words[:, : T // 2])
        nc.sync.dma_start(out=key_words[:, T // 2 :].bitcast(I32), in_=words[:, T // 2 :])
        q_raw = sb.tile([P, PACK, Q], F32, name="q_raw")
        nc.sync.dma_start(out=q_raw[:], in_=query.rearrange("(p j) q -> p j q", j=PACK))
        list_b = sb.tile([P, I // 16], U16, name="list_b")
        nc.sync.dma_start(list_b[:], offs2)
        list_a = sb.tile([P, I // 16], U16, name="list_a")
        nc.sync.dma_start(list_a[:], offs)
        lam_sb = sb.tile([P, 1], F32, name="lam_sb")
        nc.sync.dma_start(out=lam_sb[:], in_=lam)
        old_sb = sb.tile([P, T], F32, name="old_sb")
        nc.sync.dma_start(out=old_sb[:], in_=old)
        list_f = sb.tile([P, I // 16], U16, name="list_f")
        nc.sync.dma_start(list_f[:], offs3)

        f1 = sb.tile([P, T], F32, name="f1")
        nc.gpsimd.memset(f1[:], 0.0)
        warm = sb.tile([P, 1], F32, name="warm")
        nc.vector.memset(warm[:], 0.0)
        warm_out = sb.tile([P, 1], F32, name="warm_out")
        nc.scalar.activation(warm_out[:], warm[:], ACT.Sigmoid)

        def quantise(raw, name, cast):
            grouped = sb.tile(
                [P, Q, PACK], BF16, name=name + "_grouped", tag=name + "_grouped", align_bytes=64
            )
            cast(
                grouped[:].rearrange("p (c i) t -> p c t i", i=4),
                raw[:].rearrange("p t (c i) -> p c t i", i=4),
            )
            codes = sb.tile([P, Q], U32, name=name + "_codes", align_bytes=64)
            scale = sb.tile([P, Q], U8, name=name + "_scale", align_bytes=64)
            nc.vector.quantize_mx(
                out=codes[:].bitcast(FP8X4),
                scales=scale[:],
                in_=grouped[:].rearrange("p q t -> p (q t)"),
            )
            return codes, scale

        def scores(codes, scale, name, copies, banks):
            whole = sb.tile([P, T], F32, name=name, tag=name)
            width = T // len(copies)
            for n, copy in enumerate(copies):
                bank = ps.tile([P, width], F32, name=name + "_bank%d" % n, tag="bank%d" % banks[n])
                for col in range(0, width, N_PASS):
                    token = n * width + col
                    nc.tensor.matmul_mx(
                        out=bank[:, col : col + N_PASS],
                        lhsT=codes[:].bitcast(FP8X4),
                        lhsT_scale=scale[:],
                        rhs=key_words[:, token : token + N_PASS].bitcast(FP8X4),
                        rhs_scale=key_scale[4 * (token // N_PASS) : P, :],
                        start=True,
                        stop=True,
                    )
                copy(whole[:, n * width : (n + 1) * width], bank[:])
            return whole

        q2_codes, q2_scale = quantise(q2_raw, "q2", nc.vector.tensor_copy)
        q_codes, q_scale = quantise(q_raw, "q", nc.vector.tensor_copy)
        b_sb = scores(
            q2_codes, q2_scale, "b_sb", [nc.scalar.copy] * 4, [0, 1, 2, 3]
        )

        lo, hi = slice(0, HALF), slice(HALF, I)
        sig = sb.tile([P, I], F32, name="sig")
        nc.scalar.activation(sig[:], b_sb[:].indirect(list_b[:]), ACT.Sigmoid, scale=-1.0)
        b_listed = sb.tile([P, I], F32, name="b_listed", tag="q_grouped", align_bytes=64)
        nc.vector.tensor_copy(b_listed[:], b_sb[:].indirect(list_b[:]))

        a_sb = scores(q_codes, q_scale, "a_sb", [nc.vector.tensor_copy] * 2, [3, 2])
        a_listed = sb.tile([P, I], F32, name="a_listed")
        nc.vector.tensor_copy(a_listed[:], a_sb[:].indirect(list_a[:]))

        log_sig = sb.tile([P, I], F32, name="log_sig")
        nc.scalar.activation(log_sig[:], sig[:], ACT.Ln, bias=TINY)
        soft = sb.tile([P, I], F32, name="soft", tag="a_sb")
        den_sq = sb.tile([P, I], F32, name="den_sq")
        a_lam = sb.tile([P, I], F32, name="a_lam")
        for part in (lo, hi):
            nc.vector.scalar_tensor_tensor(
                soft[:, part], log_sig[:, part], -1.0, b_listed[:, part], ALU.mult, ALU.max
            )
        nc.vector.scalar_tensor_tensor(den_sq[:, lo], soft[:, lo], 1.0, soft[:, lo], ALU.add, ALU.mult)
        nc.vector.tensor_scalar(a_lam[:], a_listed[:], lam_sb[:], None, ALU.mult)
        nc.vector.scalar_tensor_tensor(den_sq[:, hi], soft[:, hi], 1.0, soft[:, hi], ALU.add, ALU.mult)

        inv_den = sb.tile([P, I], F32, name="inv_den")
        w = sb.tile([P, I], F32, name="w")
        for start, stop in ((0, FIRST), (FIRST, I)):
            nc.scalar.activation(
                inv_den[:, start:stop], den_sq[:, start:stop], ACT.Abs_reciprocal_sqrt, bias=0.25
            )
        nc.vector.tensor_tensor(
            f1[:].indirect(entries(list_a, 0, FIRST)), a_lam[:, :FIRST], inv_den[:, :FIRST], ALU.mult
        )
        nc.vector.tensor_tensor(w[:, lo], a_lam[:, lo], inv_den[:, lo], ALU.mult)
        nc.vector.tensor_tensor(
            f1[:].indirect(entries(list_a, FIRST, I)), a_lam[:, FIRST:], inv_den[:, FIRST:], ALU.mult
        )
        nc.vector.tensor_tensor(w[:, hi], a_lam[:, hi], inv_den[:, hi], ALU.mult)

        f2 = sb.tile([P, T], F32, name="f2")
        nc.vector.tensor_tensor(f2[:], f1[:], old_sb[:], ALU.add)

        out_lo = sb.tile([P, HALF], F32, name="out_lo")
        out_hi = sb.tile([P, HALF], F32, name="out_hi")
        f2_hi = sb.tile([P, HALF], F32, name="f2_hi")
        nc.scalar.activation(f2_hi[:], f2[:].indirect(entries(list_f, HALF, I)), ACT.Copy)
        nc.vector.tensor_tensor(
            out_lo[:], f2[:].indirect(entries(list_f, 0, HALF)), w[:, lo], ALU.mult
        )
        nc.sync.dma_start(out=out[:, lo], in_=out_lo[:])
        nc.vector.tensor_tensor(out_hi[:], f2_hi[:], w[:, hi], ALU.mult)
        nc.scalar.dma_start(out=out[:, hi], in_=out_hi[:])
